import numpy as np
import ml_dtypes


def mxq(x, axis, fmt="e4m3"):
    dtype, down = {"e4m3": (ml_dtypes.float8_e4m3fn, 7), "e5m2": (ml_dtypes.float8_e5m2, 14)}[fmt]
    v = np.moveaxis(np.asarray(x, np.float32).astype(ml_dtypes.bfloat16).astype(np.float64), axis, -1)
    blocks = v.reshape(v.shape[:-1] + (-1, 32))
    amax = np.abs(blocks).max(-1, keepdims=True)
    byte = np.maximum(np.where(amax > 0, np.frexp(amax)[1] - 1 + 127, 0) - down, 1)
    scale = np.exp2(byte - 127.0)
    codes = (blocks / scale).astype(np.float32).astype(dtype).astype(np.float64)
    return np.moveaxis((codes * scale).reshape(v.shape), -1, axis)


WIDE = False


def mx_kscale(k):
    if not WIDE:
        return np.ones(k)
    levels = np.array([10, -10, 5, -5, 0])
    if k % 512:
        return np.exp2(np.random.permutation(np.resize(levels, k // 32))).repeat(32)
    a = np.empty((k // 512, 16))
    for p in range(k // 512):
        a[p, :8] = np.random.permutation(np.resize(levels, 8))
        for g in range(8):
            far = levels[np.abs(levels - a[p, g]) >= 10]
            a[p, g + 8] = far[np.random.randint(len(far))]
    return np.exp2(a.ravel()).repeat(32)


def f64(x):
    return np.asarray(x).astype(np.float64)


def striped(idx):
    return np.tile(idx.reshape(-1, 16).T, (8, 1)).astype(np.uint16)


def unstriped(offs):
    return offs[:16].T.reshape(-1).astype(np.int64)


def pack_weight(w):
    k, n = w.shape
    w = f64(np.asarray(w, np.float32).astype(ml_dtypes.bfloat16)).reshape(k // 32, 32, n)
    amax = np.abs(w).max(1)
    byte = np.clip(np.where(amax > 0, np.frexp(amax)[1] - 1 + 127 - 7, 1), 1, 254)
    scaled = (w * np.exp2(127.0 - byte)[:, None, :]).reshape(k, n).astype(np.float32)
    words = np.ascontiguousarray(scaled.reshape(k // 512, 128, 4, n).transpose(0, 1, 3, 2)).astype(ml_dtypes.float8_e4m3fn).view(np.uint8)
    return words, np.ascontiguousarray(byte.astype(np.uint8).reshape(k // 512, 16, n))


def unpack_weight(words, scales):
    g, p, n, _ = words.shape
    vals = np.ascontiguousarray(words).view(ml_dtypes.float8_e4m3fn).astype(np.float64) * np.repeat(np.exp2(scales.astype(np.float64) - 127.0), 8, axis=1)[..., None]
    return vals.transpose(0, 1, 3, 2).reshape(g * 512, n)


def sigmoid(v):
    return 1.0 / (1.0 + np.exp(-np.maximum(v, -700.0)))

def planes(y):
    n, m = y.shape
    v = y.astype(np.float32).astype(ml_dtypes.bfloat16).astype(np.float64).reshape(n // 32, 32, m)
    top = np.abs(v).max(1)
    byte = np.clip(np.where(top > 0, np.frexp(top)[1] - 1 + 127 - 7, 1), 1, 254)
    codes = (v * np.exp2(127.0 - byte)[:, None, :]).reshape(n, m).astype(np.float32).astype(ml_dtypes.float8_e4m3fn).view(np.uint8)
    words = codes.reshape(n // 512, 128, 4, m).transpose(0, 1, 3, 2)
    return np.ascontiguousarray(words), np.ascontiguousarray(byte.astype(np.uint8).reshape(n // 512, 16, m))


K, T, S, N, H = 512, 2048, 512, 512, 512


def setup_inputs():
    n = np.random.standard_normal
    s = mx_kscale(K)[:, None]
    u = mx_kscale(S)
    packed_xT = pack_weight(n((K, T)) * s)
    return {
        "x_words": packed_xT[0],
        "x_scales": packed_xT[1],
        "wa": (n((K, H)) / np.sqrt(K) / s).astype(np.float32),
        "wb": (n((K, N)) / np.sqrt(K) / s).astype(np.float32),
        "gt": (np.random.uniform(0.5, 1.5, (S, 1)) * u[:, None]).astype(np.float32),
        "gi": (np.random.uniform(0.5, 1.5, (S, 1)) / u[:, None]).astype(np.float32),
        "offs": striped(np.random.permutation(T)[:S]),
        "val_l": striped(np.random.permutation(T)[:S]),
    }


def reference(x_words, x_scales, wa, wb, gt, gi, offs, val_l):
    xq = unpack_weight(x_words, x_scales)[:, unstriped(offs)]
    a = xq.T @ mxq(f64(wa), 0, "e4m3")
    z = f64(gt) * sigmoid(a)
    x_val_l = unpack_weight(x_words, x_scales)[:, unstriped(val_l)]
    b = x_val_l.T @ mxq(f64(wb), 0, "e4m3")
    z2 = f64(gi) * b
    out_0 = 0.0625 * ((mxq(z, 0, "e4m3").T @ mxq(z2, 0, "e4m3")))
    return (out_0,) + planes(out_0)

@@ -1,0 +1,242 @@
+from contextlib import ExitStack
+
+import concourse.mybir as mybir
+
+K, T, S, H, N = 512, 2048, 512, 512, 512
+FLOPS = 2 * (K * S * H + K * S * N + S * H * N)
+
+F32 = mybir.dt.float32
+BF16 = mybir.dt.bfloat16
+I32 = mybir.dt.int32
+U32 = mybir.dt.uint32
+U16 = mybir.dt.uint16
+U8 = mybir.dt.uint8
+FP8X4 = mybir.dt.float8_e4m3fn_x4
+MULT = mybir.AluOpType.mult
+SIGMOID = mybir.ActivationFunctionType.Sigmoid
+COPY = mybir.ActivationFunctionType.Copy
+
+P = 128
+PACK = 4
+CHUNK = 128
+CHUNKS = 4
+HALF = 256
+OUT_SCALE = 0.0625
+
+
+def tile_picked_toklearn_sigmoid_po_kernel(tc, x_words, x_scales, wa, wb, gt, gi, offs, val_l, out_0, out_1, out_2):
+    nc = tc.nc
+    with ExitStack() as ctx:
+        keep = ctx.enter_context(tc.tile_pool(name="keep", bufs=1))
+        psum = ctx.enter_context(tc.psum_pool(name="psum", bufs=1))
+
+        def sb(name, shape, dtype, pool=keep, tag=""):
+            return pool.tile(shape, dtype, name=name, align_bytes=64, tag=tag)
+
+        def bank(b, name):
+            return psum.tile([P, PACK, CHUNK], F32, name=name, tag="bank%d" % b)
+
+        lists = [sb("list_a", [P, S // 16], U16), sb("list_b", [P, S // 16], U16)]
+        table_words = sb("table_words", [P, T], U32)
+        table_scales = sb("table_scales", [P, T], U8)
+        ident = sb("ident", [P, P], F32)
+        gate_rows = sb("gate_rows", [P, P], F32)
+
+        nc.gpsimd.memset(table_scales[:].bitcast(I32), 0)
+        nc.gpsimd.memset(gate_rows[:], 0.0)
+        with tc.tile_pool(name="setup", bufs=1) as setup:
+            zeros = setup.tile([P, P], F32)
+            nc.gpsimd.memset(zeros[:], 0.0)
+            nc.gpsimd.affine_select(
+                out=ident[:], in_=zeros[:], compare_op=mybir.AluOpType.not_equal, fill=1.0, base=0, pattern=[[-1, P]], channel_multiplier=1
+            )
+        late = ctx.enter_context(tc.tile_pool(name="late", bufs=1))
+        w_raw = [[sb("w_raw%d%d" % (w, u), [P, PACK, HALF], F32, pool=late if w + u else keep, tag="w_raw%d%d" % (w, u)) for u in range(2)] for w in range(2)]
+
+        def load_w(w, u):
+            rows = (wa, wb)[w].rearrange("(p j) c -> p j c", j=PACK)
+            nc.sync.dma_start(out=w_raw[w][u][:], in_=rows[:, :, u * HALF : (u + 1) * HALF])
+
+        for q in range(4):
+            nc.scalar.dma_start(out=table_scales[32 * q : 32 * q + 4, :].bitcast(I32), in_=x_scales[0, 4 * q : 4 * q + 4, :].bitcast(I32))
+        nc.sync.dma_start(lists[0][:], offs)
+        nc.sync.dma_start(lists[1][:], val_l)
+        nc.sync.dma_start(out=table_words[:].bitcast(I32), in_=x_words[0].rearrange("p c r -> p (c r)").bitcast(I32))
+        load_w(0, 0)
+        load_w(0, 1)
+        for g, gate in enumerate((gt, gi)):
+            nc.sync.dma_start(
+                out=gate_rows[PACK * g : PACK * (g + 1), :].rearrange("t (q r) -> t q r", r=8),
+                in_=gate.rearrange("(q t r) o -> t q (r o)", t=PACK, r=8),
+            )
+        load_w(1, 0)
+        load_w(1, 1)
+
+        warm = sb("warm", [P, 1], F32)
+        nc.scalar.activation(warm[:], ident[:, 0:1], SIGMOID)
+
+        picked_scales = [sb("picked_scales%d" % w, [P, S], U8, tag="picked%d" % w) for w in range(2)]
+        dealt_scales = [sb("dealt_scales%d" % w, [P, S], U8) for w in range(2)]
+        for w in range(2):
+            nc.vector.tensor_copy(picked_scales[w][:], table_scales[:].indirect(lists[w][:]))
+        for w in range(2):
+            nc.vector.tensor_copy(
+                dealt_scales[w][:].bitcast(I32).rearrange("p (t q e) -> p t q e", t=PACK, e=2),
+                picked_scales[w][:].bitcast(I32).rearrange("p (q t e) -> p t q e", t=PACK, e=2),
+            )
+        picked_words = []
+
+        def gather_words(w, tag):
+            picked_words.append(sb("picked_words%d" % w, [P, S], U32, tag=tag))
+            nc.vector.tensor_copy(picked_words[w][:].rearrange("p (t q r) -> p q t r", t=PACK, r=8), table_words[:].indirect(lists[w][:]))
+
+        gather_words(0, "picked0")
+
+        gate_bank = bank(7, "gate_bank")
+        nc.tensor.transpose(gate_bank[:, 0, :], gate_rows[:], ident[:])
+        gates = sb("gates", [P, 2 * PACK], F32)
+        nc.scalar.copy(gates[:], gate_bank[:, 0, 0 : 2 * PACK])
+
+        def weave(copy, dst, src):
+            copy(dst.rearrange("p (c i) j -> p c j i", i=4), src.rearrange("p j (c i) -> p c j i", i=4))
+
+        def quant(codes, scales, src):
+            nc.vector.quantize_mx(out=codes.bitcast(FP8X4), scales=scales, in_=src)
+
+        wa_bf = [sb("wa_bf%d" % u, [P, HALF, PACK], BF16, tag="wa_bf%d" % u) for u in range(2)]
+        wa_codes = [sb("wa_codes%d" % u, [P, HALF], U32, tag=("picked1", "")[u]) for u in range(2)]
+        wa_scales = [sb("wa_scales%d" % u, [P, HALF], U8) for u in range(2)]
+        wb_bf = {}
+        pair_tags = ("w_raw01", "sig23")
+        wb_codes = [sb("wb_codes%d" % c, [P, CHUNK], U32) for c in range(CHUNKS)]
+        wb_scales = [sb("wb_scales%d" % c, [P, CHUNK], U8) for c in range(CHUNKS)]
+
+        def half_cols(c):
+            return slice((c % 2) * CHUNK, (c % 2 + 1) * CHUNK)
+
+        def weave_wa(u):
+            weave(nc.scalar.copy, wa_bf[u][:], w_raw[0][u][:])
+
+        def quant_wa(u):
+            quant(wa_codes[u][:], wa_scales[u][:], wa_bf[u][:].rearrange("p c j -> p (c j)"))
+
+        def weave_wb(c):
+            if c % 2 == 0:
+                pair = sb("wb_bf%d" % c, [P, 2, CHUNK, PACK], BF16, pool=late, tag=pair_tags[c // 2])
+                wb_bf[c], wb_bf[c + 1] = pair[:, 0], pair[:, 1]
+            weave(nc.scalar.copy, wb_bf[c], w_raw[1][c // 2][:, :, half_cols(c)])
+
+        def quant_wb(c):
+            quant(wb_codes[c][:], wb_scales[c][:], wb_bf[c].rearrange("p c j -> p (c j)"))
+
+        def four_passes(acc, st_codes, st_scales, mv_codes, mv_scales):
+            for t in range(PACK):
+                cols = slice(t * P, (t + 1) * P)
+                nc.tensor.matmul_mx(
+                    out=acc[:, t, :],
+                    lhsT=st_codes[:, cols].bitcast(FP8X4),
+                    lhsT_scale=st_scales[:, cols],
+                    rhs=mv_codes.bitcast(FP8X4),
+                    rhs_scale=mv_scales,
+                    start=True,
+                    stop=True,
+                )
+
+        def first_product(w, c):
+            acc = bank(CHUNKS * w + c, "acc%d%d" % (w, c))
+            if w == 0:
+                codes, scales = wa_codes[c // 2][:, half_cols(c)], wa_scales[c // 2][:, half_cols(c)]
+            else:
+                codes, scales = wb_codes[c][:], wb_scales[c][:]
+            four_passes(acc, picked_words[w][:], dealt_scales[w][:], codes, scales)
+            return acc
+
+        sig = {}
+        z_bf = sb("z_bf", [P, PACK, P, PACK], BF16)
+        z_codes = sb("z_codes", [P, H], U32)
+        z_scales = sb("z_scales", [P, H], U8)
+
+        def sigmoid_chunk(c):
+            acc = first_product(0, c)
+            if c % 2 == 0:
+                pair = sb("sig%d" % c, [P, 2, PACK, 32, PACK], F32, pool=late, tag=pair_tags[c // 2])
+                sig[c], sig[c + 1] = pair[:, 0], pair[:, 1]
+            nc.scalar.activation(sig[c], acc[:].rearrange("p t (m d) -> p d m t", d=PACK), SIGMOID)
+
+        def gate_z(c):
+            nc.vector.tensor_tensor(
+                z_bf[:, :, 32 * c : 32 * (c + 1), :], sig[c], gates[:, 0:PACK].unsqueeze(1).unsqueeze(1).to_broadcast([P, PACK, 32, PACK]), MULT
+            )
+
+        v_bf = [sb("v_bf%d" % c, [P, CHUNK, PACK], BF16) for c in range(CHUNKS)]
+        v_codes = [sb("v_codes%d" % c, [P, CHUNK], U32) for c in range(CHUNKS)]
+        v_scales = [sb("v_scales%d" % c, [P, CHUNK], U8) for c in range(CHUNKS)]
+
+        b_acc = {}
+
+        def values(c):
+            quant_wb(c)
+            b_acc[c] = first_product(1, c)
+
+        def gate_v(c):
+            acc = b_acc[c]
+            nc.vector.tensor_tensor(
+                v_bf[c][:], acc[:].rearrange("p t n -> p n t"), gates[:, PACK : 2 * PACK].unsqueeze(1).to_broadcast([P, CHUNK, PACK]), MULT
+            )
+
+        def quant_v(c):
+            quant(v_codes[c][:], v_scales[c][:], v_bf[c][:].rearrange("p n t -> p (n t)"))
+
+        y = [sb("y%d" % c, [P, PACK, CHUNK], F32) for c in range(CHUNKS)]
+        y_bf = [sb("y_bf%d" % c, [P, CHUNK, PACK], BF16) for c in range(CHUNKS)]
+        y_codes = sb("y_codes", [P, N], U32)
+        y_scales = sb("y_scales", [P, N], U8)
+        out_rows = out_0.rearrange("(p d) n -> p d n", d=PACK)
+
+        def last_product(c):
+            acc = bank(c, "out_acc%d" % c)
+            four_passes(acc, z_codes[:], z_scales[:], v_codes[c][:], v_scales[c][:])
+            nc.scalar.activation(y[c][:], acc[:], COPY, scale=OUT_SCALE)
+            nc.sync.dma_start(out=out_rows[:, :, c * CHUNK : (c + 1) * CHUNK], in_=y[c][:])
+
+        def weave_y(c):
+            weave(nc.vector.tensor_copy, y_bf[c][:], y[c][:])
+
+        def quant_y(c):
+            cols = slice(c * CHUNK, (c + 1) * CHUNK)
+            quant(y_codes[:, cols], y_scales[:, cols], y_bf[c][:].rearrange("p n d -> p (n d)"))
+
+        weave_wa(0)
+        quant_wa(0)
+        gather_words(1, "wa_bf0")
+        weave_wa(1)
+        quant_wa(1)
+        for c in range(CHUNKS):
+            sigmoid_chunk(c)
+            gate_z(c)
+        for c in range(CHUNKS):
+            weave_wb(c)
+        values(0)
+        quant(z_codes[:], z_scales[:], z_bf[:].rearrange("p d m t -> p (d m t)"))
+        values(1)
+        for c in range(CHUNKS):
+            gate_v(c)
+            if c + 2 < CHUNKS:
+                values(c + 2)
+            if c > 0:
+                quant_v(c - 1)
+                last_product(c - 1)
+        quant_v(CHUNKS - 1)
+        last_product(CHUNKS - 1)
+        words_out = out_1[0].rearrange("p n r -> p (n r)").bitcast(I32)
+        for c in range(CHUNKS):
+            weave_y(c)
+            if c > 0:
+                quant_y(c - 1)
+        early = (CHUNKS - 1) * CHUNK
+        nc.sync.dma_start(out=words_out[:, :early], in_=y_codes[:, :early].bitcast(I32))
+        quant_y(CHUNKS - 1)
+        nc.sync.dma_start(out=words_out[:, early:], in_=y_codes[:, early:].bitcast(I32))
+        for q in range(4):
+            eng = nc.scalar if q % 2 else nc.sync
+            eng.dma_start(out=out_2[0, 4 * q : 4 * q + 4, :].bitcast(I32), in_=y_scales[32 * q : 32 * q + 4, :].bitcast(I32))

@@ -37,13 +37,11 @@ def tile_picked_toklearn_sigmoid_po_kernel(tc, x_words, x_scales, wa, wb, gt, gi
             return psum.tile([P, PACK, CHUNK], F32, name=name, tag="bank%d" % b)
 
         lists = [sb("list_a", [P, S // 16], U16), sb("list_b", [P, S // 16], U16)]
-        table_words = sb("table_words", [P, T], U32)
         table_scales = sb("table_scales", [P, T], U8)
         ident = sb("ident", [P, P], F32)
-        gate_rows = sb("gate_rows", [P, P], F32)
 
-        nc.gpsimd.memset(table_scales[:].bitcast(I32), 0)
-        nc.gpsimd.memset(gate_rows[:], 0.0)
+        nc.gpsimd.memset(table_scales[:, : T // 2].bitcast(I32), 0)
+        nc.vector.memset(table_scales[:, T // 2 :].bitcast(I32), 0)
         with tc.tile_pool(name="setup", bufs=1) as setup:
             zeros = setup.tile([P, P], F32)
             nc.gpsimd.memset(zeros[:], 0.0)
@@ -51,26 +49,28 @@ def tile_picked_toklearn_sigmoid_po_kernel(tc, x_words, x_scales, wa, wb, gt, gi
                 out=ident[:], in_=zeros[:], compare_op=mybir.AluOpType.not_equal, fill=1.0, base=0, pattern=[[-1, P]], channel_multiplier=1
             )
         late = ctx.enter_context(tc.tile_pool(name="late", bufs=1))
-        w_raw = [[sb("w_raw%d%d" % (w, u), [P, PACK, HALF], F32, pool=late if w + u else keep, tag="w_raw%d%d" % (w, u)) for u in range(2)] for w in range(2)]
+        gate_rows = sb("gate_rows", [P, P], F32)
+        nc.gpsimd.memset(gate_rows[:], 0.0)
+        table_words = sb("table_words", [P, T], U32, pool=late)
+        wa_raw = [sb("wa_raw0", [P, PACK, HALF], F32, tag="first_raw"), sb("wa_raw1", [P, PACK, HALF], F32, pool=late, tag="w_raw01")]
 
-        def load_w(w, u):
-            rows = (wa, wb)[w].rearrange("(p j) c -> p j c", j=PACK)
-            nc.sync.dma_start(out=w_raw[w][u][:], in_=rows[:, :, u * HALF : (u + 1) * HALF])
+        def load_wa(u):
+            nc.sync.dma_start(out=wa_raw[u][:], in_=wa.rearrange("(p j) c -> p j c", j=PACK)[:, :, u * HALF : (u + 1) * HALF])
 
-        for q in range(4):
-            nc.scalar.dma_start(out=table_scales[32 * q : 32 * q + 4, :].bitcast(I32), in_=x_scales[0, 4 * q : 4 * q + 4, :].bitcast(I32))
         nc.sync.dma_start(lists[0][:], offs)
         nc.sync.dma_start(lists[1][:], val_l)
+        load_wa(0)
+        for q in range(4):
+            nc.sync.dma_start(out=table_scales[32 * q : 32 * q + 4, :].bitcast(I32), in_=x_scales[0, 4 * q : 4 * q + 4, :].bitcast(I32))
         nc.sync.dma_start(out=table_words[:].bitcast(I32), in_=x_words[0].rearrange("p c r -> p (c r)").bitcast(I32))
-        load_w(0, 0)
-        load_w(0, 1)
+        load_wa(1)
+        wb_raw = sb("wb_raw", [P, PACK, N], F32, pool=late)
+        nc.sync.dma_start(out=wb_raw[:], in_=wb.rearrange("(p j) c -> p j c", j=PACK))
         for g, gate in enumerate((gt, gi)):
-            nc.sync.dma_start(
+            nc.gpsimd.dma_start(
                 out=gate_rows[PACK * g : PACK * (g + 1), :].rearrange("t (q r) -> t q r", r=8),
                 in_=gate.rearrange("(q t r) o -> t q (r o)", t=PACK, r=8),
             )
-        load_w(1, 0)
-        load_w(1, 1)
 
         warm = sb("warm", [P, 1], F32)
         nc.scalar.activation(warm[:], ident[:, 0:1], SIGMOID)
@@ -115,7 +115,7 @@ def tile_picked_toklearn_sigmoid_po_kernel(tc, x_words, x_scales, wa, wb, gt, gi
             return slice((c % 2) * CHUNK, (c % 2 + 1) * CHUNK)
 
         def weave_wa(u):
-            weave(nc.scalar.copy, wa_bf[u][:], w_raw[0][u][:])
+            weave(nc.scalar.copy, wa_bf[u][:], wa_raw[u][:])
 
         def quant_wa(u):
             quant(wa_codes[u][:], wa_scales[u][:], wa_bf[u][:].rearrange("p c j -> p (c j)"))
@@ -124,7 +124,7 @@ def tile_picked_toklearn_sigmoid_po_kernel(tc, x_words, x_scales, wa, wb, gt, gi
             if c % 2 == 0:
                 pair = sb("wb_bf%d" % c, [P, 2, CHUNK, PACK], BF16, pool=late, tag=pair_tags[c // 2])
                 wb_bf[c], wb_bf[c + 1] = pair[:, 0], pair[:, 1]
-            weave(nc.scalar.copy, wb_bf[c], w_raw[1][c // 2][:, :, half_cols(c)])
+            weave(nc.scalar.copy, wb_bf[c], wb_raw[:, :, c * CHUNK : (c + 1) * CHUNK])
 
         def quant_wb(c):
             quant(wb_codes[c][:], wb_scales[c][:], wb_bf[c].rearrange("p c j -> p (c j)"))
@@ -168,7 +168,8 @@ def tile_picked_toklearn_sigmoid_po_kernel(tc, x_words, x_scales, wa, wb, gt, gi
                 z_bf[:, :, 32 * c : 32 * (c + 1), :], sig[c], gates[:, 0:PACK].unsqueeze(1).unsqueeze(1).to_broadcast([P, PACK, 32, PACK]), MULT
             )
 
-        v_bf = [sb("v_bf%d" % c, [P, CHUNK, PACK], BF16) for c in range(CHUNKS)]
+        v_pairs = [sb("v_bf%d" % u, [P, 2, CHUNK, PACK], BF16, tag="v_bf%d" % u) for u in range(2)]
+        v_bf = [v_pairs[c // 2][:, c % 2] for c in range(CHUNKS)]
         v_codes = [sb("v_codes%d" % c, [P, CHUNK], U32) for c in range(CHUNKS)]
         v_scales = [sb("v_scales%d" % c, [P, CHUNK], U8) for c in range(CHUNKS)]
 
@@ -181,14 +182,13 @@ def tile_picked_toklearn_sigmoid_po_kernel(tc, x_words, x_scales, wa, wb, gt, gi
         def gate_v(c):
             acc = b_acc[c]
             nc.vector.tensor_tensor(
-                v_bf[c][:], acc[:].rearrange("p t n -> p n t"), gates[:, PACK : 2 * PACK].unsqueeze(1).to_broadcast([P, CHUNK, PACK]), MULT
+                v_bf[c], acc[:].rearrange("p t n -> p n t"), gates[:, PACK : 2 * PACK].unsqueeze(1).to_broadcast([P, CHUNK, PACK]), MULT
             )
 
         def quant_v(c):
-            quant(v_codes[c][:], v_scales[c][:], v_bf[c][:].rearrange("p n t -> p (n t)"))
+            quant(v_codes[c][:], v_scales[c][:], v_bf[c].rearrange("p n t -> p (n t)"))
 
-        y = [sb("y%d" % c, [P, PACK, CHUNK], F32) for c in range(CHUNKS)]
-        y_bf = [sb("y_bf%d" % c, [P, CHUNK, PACK], BF16) for c in range(CHUNKS)]
+        y = sb("y", [P, PACK, N], F32)
         y_codes = sb("y_codes", [P, N], U32)
         y_scales = sb("y_scales", [P, N], U8)
         out_rows = out_0.rearrange("(p d) n -> p d n", d=PACK)
@@ -196,16 +196,22 @@ def tile_picked_toklearn_sigmoid_po_kernel(tc, x_words, x_scales, wa, wb, gt, gi
         def last_product(c):
             acc = bank(c, "out_acc%d" % c)
             four_passes(acc, z_codes[:], z_scales[:], v_codes[c][:], v_scales[c][:])
-            nc.scalar.activation(y[c][:], acc[:], COPY, scale=OUT_SCALE)
-            nc.sync.dma_start(out=out_rows[:, :, c * CHUNK : (c + 1) * CHUNK], in_=y[c][:])
-
-        def weave_y(c):
-            weave(nc.vector.tensor_copy, y_bf[c][:], y[c][:])
-
-        def quant_y(c):
             cols = slice(c * CHUNK, (c + 1) * CHUNK)
-            quant(y_codes[:, cols], y_scales[:, cols], y_bf[c][:].rearrange("p n d -> p (n d)"))
+            nc.scalar.activation(y[:, :, cols], acc[:], COPY, scale=OUT_SCALE)
+            nc.sync.dma_start(out=out_rows[:, :, cols], in_=y[:, :, cols])
 
+        y_bf = {}
+
+        def weave_y(start, width, tag):
+            y_bf[start] = sb("y_bf%d" % start, [P, width, PACK], BF16, tag=tag)
+            weave(nc.vector.tensor_copy, y_bf[start][:], y[:, :, start : start + width])
+
+        def quant_y(start, width):
+            cols = slice(start, start + width)
+            quant(y_codes[:, cols], y_scales[:, cols], y_bf[start][:].rearrange("p n d -> p (n d)"))
+            nc.sync.dma_start(out=words_out[:, cols], in_=y_codes[:, cols].bitcast(I32))
+
+        words_out = out_1[0].rearrange("p n r -> p (n r)").bitcast(I32)
         weave_wa(0)
         quant_wa(0)
         gather_words(1, "wa_bf0")
@@ -228,15 +234,12 @@ def tile_picked_toklearn_sigmoid_po_kernel(tc, x_words, x_scales, wa, wb, gt, gi
                 last_product(c - 1)
         quant_v(CHUNKS - 1)
         last_product(CHUNKS - 1)
-        words_out = out_1[0].rearrange("p n r -> p (n r)").bitcast(I32)
-        for c in range(CHUNKS):
-            weave_y(c)
-            if c > 0:
-                quant_y(c - 1)
-        early = (CHUNKS - 1) * CHUNK
-        nc.sync.dma_start(out=words_out[:, :early], in_=y_codes[:, :early].bitcast(I32))
-        quant_y(CHUNKS - 1)
-        nc.sync.dma_start(out=words_out[:, early:], in_=y_codes[:, early:].bitcast(I32))
+        weave_y(0, HALF, "v_bf1")
+        weave_y(HALF, CHUNK, "")
+        quant_y(0, HALF)
+        weave_y(HALF + CHUNK, CHUNK, "")
+        quant_y(HALF, CHUNK)
+        quant_y(HALF + CHUNK, CHUNK)
         for q in range(4):
             eng = nc.scalar if q % 2 else nc.sync
             eng.dma_start(out=out_2[0, 4 * q : 4 * q + 4, :].bitcast(I32), in_=y_scales[32 * q : 32 * q + 4, :].bitcast(I32))

@@ -18,9 +18,14 @@ COPY = mybir.ActivationFunctionType.Copy
 
 P = 128
 PACK = 4
+RUN = 8
+QUADRANT = 32
+SCALE_ROWS = 4
+LIST_ROWS = 16
+LINE = 4
 CHUNK = 128
 CHUNKS = 4
-HALF = 256
+HALF = 2 * CHUNK
 OUT_SCALE = 0.0625
 
 
@@ -36,7 +41,7 @@ def tile_picked_toklearn_sigmoid_po_kernel(tc, x_words, x_scales, wa, wb, gt, gi
         def bank(b, name):
             return psum.tile([P, PACK, CHUNK], F32, name=name, tag="bank%d" % b)
 
-        lists = [sb("list_a", [P, S // 16], U16), sb("list_b", [P, S // 16], U16)]
+        lists = [sb("list_a", [P, S // LIST_ROWS], U16), sb("list_b", [P, S // LIST_ROWS], U16)]
         table_scales = sb("table_scales", [P, T], U8)
         ident = sb("ident", [P, P], F32)
 
@@ -52,7 +57,8 @@ def tile_picked_toklearn_sigmoid_po_kernel(tc, x_words, x_scales, wa, wb, gt, gi
         gate_rows = sb("gate_rows", [P, P], F32)
         nc.gpsimd.memset(gate_rows[:], 0.0)
         table_words = sb("table_words", [P, T], U32, pool=late)
-        wa_raw = [sb("wa_raw0", [P, PACK, HALF], F32, tag="first_raw"), sb("wa_raw1", [P, PACK, HALF], F32, pool=late, tag="w_raw01")]
+        pair_tags = ("pair0", "pair1")
+        wa_raw = [sb("wa_raw0", [P, PACK, HALF], F32), sb("wa_raw1", [P, PACK, HALF], F32, pool=late, tag=pair_tags[0])]
 
         def load_wa(u):
             nc.sync.dma_start(out=wa_raw[u][:], in_=wa.rearrange("(p j) c -> p j c", j=PACK)[:, :, u * HALF : (u + 1) * HALF])
@@ -60,59 +66,60 @@ def tile_picked_toklearn_sigmoid_po_kernel(tc, x_words, x_scales, wa, wb, gt, gi
         nc.sync.dma_start(lists[0][:], offs)
         nc.sync.dma_start(lists[1][:], val_l)
         load_wa(0)
-        for q in range(4):
-            nc.sync.dma_start(out=table_scales[32 * q : 32 * q + 4, :].bitcast(I32), in_=x_scales[0, 4 * q : 4 * q + 4, :].bitcast(I32))
+        for q in range(P // QUADRANT):
+            nc.sync.dma_start(
+                out=table_scales[QUADRANT * q : QUADRANT * q + SCALE_ROWS, :].bitcast(I32),
+                in_=x_scales[0, SCALE_ROWS * q : SCALE_ROWS * (q + 1), :].bitcast(I32),
+            )
         nc.sync.dma_start(out=table_words[:].bitcast(I32), in_=x_words[0].rearrange("p c r -> p (c r)").bitcast(I32))
         load_wa(1)
         wb_raw = sb("wb_raw", [P, PACK, N], F32, pool=late)
         nc.sync.dma_start(out=wb_raw[:], in_=wb.rearrange("(p j) c -> p j c", j=PACK))
         for g, gate in enumerate((gt, gi)):
             nc.gpsimd.dma_start(
-                out=gate_rows[PACK * g : PACK * (g + 1), :].rearrange("t (q r) -> t q r", r=8),
-                in_=gate.rearrange("(q t r) o -> t q (r o)", t=PACK, r=8),
+                out=gate_rows[PACK * g : PACK * (g + 1), :].rearrange("t (q r) -> t q r", r=RUN),
+                in_=gate.rearrange("(q t r) o -> t q (r o)", t=PACK, r=RUN),
             )
 
         warm = sb("warm", [P, 1], F32)
         nc.scalar.activation(warm[:], ident[:, 0:1], SIGMOID)
 
-        picked_scales = [sb("picked_scales%d" % w, [P, S], U8, tag="picked%d" % w) for w in range(2)]
+        picked_scales = [sb("picked_scales%d" % w, [P, S], U8, tag="picked_scales%d" % w) for w in range(2)]
         dealt_scales = [sb("dealt_scales%d" % w, [P, S], U8) for w in range(2)]
         for w in range(2):
             nc.vector.tensor_copy(picked_scales[w][:], table_scales[:].indirect(lists[w][:]))
         for w in range(2):
             nc.vector.tensor_copy(
-                dealt_scales[w][:].bitcast(I32).rearrange("p (t q e) -> p t q e", t=PACK, e=2),
-                picked_scales[w][:].bitcast(I32).rearrange("p (q t e) -> p t q e", t=PACK, e=2),
+                dealt_scales[w][:].bitcast(I32).rearrange("p (t q e) -> p t q e", t=PACK, e=RUN // PACK),
+                picked_scales[w][:].bitcast(I32).rearrange("p (q t e) -> p t q e", t=PACK, e=RUN // PACK),
             )
-        picked_words = []
+        picked_words = [sb("picked_words%d" % w, [P, S], U32) for w in range(2)]
 
-        def gather_words(w, tag):
-            picked_words.append(sb("picked_words%d" % w, [P, S], U32, tag=tag))
-            nc.vector.tensor_copy(picked_words[w][:].rearrange("p (t q r) -> p q t r", t=PACK, r=8), table_words[:].indirect(lists[w][:]))
+        def gather_words(w):
+            nc.vector.tensor_copy(picked_words[w][:].rearrange("p (t q r) -> p q t r", t=PACK, r=RUN), table_words[:].indirect(lists[w][:]))
 
-        gather_words(0, "picked0")
+        gather_words(0)
 
-        gate_bank = bank(7, "gate_bank")
+        gate_bank = bank(2 * CHUNKS - 1, "gate_bank")
         nc.tensor.transpose(gate_bank[:, 0, :], gate_rows[:], ident[:])
         gates = sb("gates", [P, 2 * PACK], F32)
         nc.scalar.copy(gates[:], gate_bank[:, 0, 0 : 2 * PACK])
 
         def weave(copy, dst, src):
-            copy(dst.rearrange("p (c i) j -> p c j i", i=4), src.rearrange("p j (c i) -> p c j i", i=4))
+            copy(dst.rearrange("p (c i) j -> p c j i", i=LINE), src.rearrange("p j (c i) -> p c j i", i=LINE))
 
         def quant(codes, scales, src):
             nc.vector.quantize_mx(out=codes.bitcast(FP8X4), scales=scales, in_=src)
 
-        wa_bf = [sb("wa_bf%d" % u, [P, HALF, PACK], BF16, tag="wa_bf%d" % u) for u in range(2)]
-        wa_codes = [sb("wa_codes%d" % u, [P, HALF], U32, tag=("picked1", "")[u]) for u in range(2)]
+        wa_bf = [sb("wa_bf%d" % u, [P, HALF, PACK], BF16) for u in range(2)]
+        wa_codes = [sb("wa_codes0", [P, HALF], U32, tag="picked_scales0"), sb("wa_codes1", [P, HALF], U32)]
         wa_scales = [sb("wa_scales%d" % u, [P, HALF], U8) for u in range(2)]
         wb_bf = {}
-        pair_tags = ("w_raw01", "sig23")
         wb_codes = [sb("wb_codes%d" % c, [P, CHUNK], U32) for c in range(CHUNKS)]
         wb_scales = [sb("wb_scales%d" % c, [P, CHUNK], U8) for c in range(CHUNKS)]
 
-        def half_cols(c):
-            return slice((c % 2) * CHUNK, (c % 2 + 1) * CHUNK)
+        def chunk_cols(c):
+            return slice(c * CHUNK, (c + 1) * CHUNK)
 
         def weave_wa(u):
             weave(nc.scalar.copy, wa_bf[u][:], wa_raw[u][:])
@@ -124,69 +131,62 @@ def tile_picked_toklearn_sigmoid_po_kernel(tc, x_words, x_scales, wa, wb, gt, gi
             if c % 2 == 0:
                 pair = sb("wb_bf%d" % c, [P, 2, CHUNK, PACK], BF16, pool=late, tag=pair_tags[c // 2])
                 wb_bf[c], wb_bf[c + 1] = pair[:, 0], pair[:, 1]
-            weave(nc.scalar.copy, wb_bf[c], wb_raw[:, :, c * CHUNK : (c + 1) * CHUNK])
+            weave(nc.scalar.copy, wb_bf[c], wb_raw[:, :, chunk_cols(c)])
 
-        def quant_wb(c):
-            quant(wb_codes[c][:], wb_scales[c][:], wb_bf[c].rearrange("p c j -> p (c j)"))
-
-        def four_passes(acc, st_codes, st_scales, mv_codes, mv_scales):
-            for t in range(PACK):
-                cols = slice(t * P, (t + 1) * P)
+        def four_passes(acc, stationary_codes, stationary_scales, moving_codes, moving_scales):
+            for i in range(PACK):
+                cols = slice(i * P, (i + 1) * P)
                 nc.tensor.matmul_mx(
-                    out=acc[:, t, :],
-                    lhsT=st_codes[:, cols].bitcast(FP8X4),
-                    lhsT_scale=st_scales[:, cols],
-                    rhs=mv_codes.bitcast(FP8X4),
-                    rhs_scale=mv_scales,
+                    out=acc[:, i, :],
+                    lhsT=stationary_codes[:, cols].bitcast(FP8X4),
+                    lhsT_scale=stationary_scales[:, cols],
+                    rhs=moving_codes.bitcast(FP8X4),
+                    rhs_scale=moving_scales,
                     start=True,
                     stop=True,
                 )
-
-        def first_product(w, c):
-            acc = bank(CHUNKS * w + c, "acc%d%d" % (w, c))
-            if w == 0:
-                codes, scales = wa_codes[c // 2][:, half_cols(c)], wa_scales[c // 2][:, half_cols(c)]
-            else:
-                codes, scales = wb_codes[c][:], wb_scales[c][:]
-            four_passes(acc, picked_words[w][:], dealt_scales[w][:], codes, scales)
-            return acc
 
         sig = {}
         z_bf = sb("z_bf", [P, PACK, P, PACK], BF16)
         z_codes = sb("z_codes", [P, H], U32)
         z_scales = sb("z_scales", [P, H], U8)
+        maps = CHUNK // PACK
 
         def sigmoid_chunk(c):
-            acc = first_product(0, c)
+            acc = bank(c, "a_acc%d" % c)
+            cols = chunk_cols(c % 2)
+            four_passes(acc, picked_words[0][:], dealt_scales[0][:], wa_codes[c // 2][:, cols], wa_scales[c // 2][:, cols])
             if c % 2 == 0:
-                pair = sb("sig%d" % c, [P, 2, PACK, 32, PACK], F32, pool=late, tag=pair_tags[c // 2])
+                pair = sb("sig%d" % c, [P, 2, PACK, maps, PACK], F32, pool=late, tag=pair_tags[c // 2])
                 sig[c], sig[c + 1] = pair[:, 0], pair[:, 1]
             nc.scalar.activation(sig[c], acc[:].rearrange("p t (m d) -> p d m t", d=PACK), SIGMOID)
 
         def gate_z(c):
             nc.vector.tensor_tensor(
-                z_bf[:, :, 32 * c : 32 * (c + 1), :], sig[c], gates[:, 0:PACK].unsqueeze(1).unsqueeze(1).to_broadcast([P, PACK, 32, PACK]), MULT
+                z_bf[:, :, maps * c : maps * (c + 1), :],
+                sig[c],
+                gates[:, 0:PACK].unsqueeze(1).unsqueeze(1).to_broadcast([P, PACK, maps, PACK]),
+                MULT,
             )
 
-        v_pairs = [sb("v_bf%d" % u, [P, 2, CHUNK, PACK], BF16, tag="v_bf%d" % u) for u in range(2)]
-        v_bf = [v_pairs[c // 2][:, c % 2] for c in range(CHUNKS)]
-        v_codes = [sb("v_codes%d" % c, [P, CHUNK], U32) for c in range(CHUNKS)]
-        v_scales = [sb("v_scales%d" % c, [P, CHUNK], U8) for c in range(CHUNKS)]
-
+        z2_pairs = [sb("z2_bf%d" % u, [P, 2, CHUNK, PACK], BF16, tag="z2_bf%d" % u) for u in range(2)]
+        z2_bf = [z2_pairs[c // 2][:, c % 2] for c in range(CHUNKS)]
+        z2_codes = [sb("z2_codes%d" % c, [P, CHUNK], U32) for c in range(CHUNKS)]
+        z2_scales = [sb("z2_scales%d" % c, [P, CHUNK], U8) for c in range(CHUNKS)]
         b_acc = {}
 
-        def values(c):
-            quant_wb(c)
-            b_acc[c] = first_product(1, c)
+        def product_b(c):
+            quant(wb_codes[c][:], wb_scales[c][:], wb_bf[c].rearrange("p c j -> p (c j)"))
+            b_acc[c] = bank(CHUNKS + c, "b_acc%d" % c)
+            four_passes(b_acc[c], picked_words[1][:], dealt_scales[1][:], wb_codes[c][:], wb_scales[c][:])
 
-        def gate_v(c):
-            acc = b_acc[c]
+        def gate_z2(c):
             nc.vector.tensor_tensor(
-                v_bf[c], acc[:].rearrange("p t n -> p n t"), gates[:, PACK : 2 * PACK].unsqueeze(1).to_broadcast([P, CHUNK, PACK]), MULT
+                z2_bf[c],
+                b_acc[c][:].rearrange("p t n -> p n t"),
+                gates[:, PACK : 2 * PACK].unsqueeze(1).to_broadcast([P, CHUNK, PACK]),
+                MULT,
             )
-
-        def quant_v(c):
-            quant(v_codes[c][:], v_scales[c][:], v_bf[c].rearrange("p n t -> p (n t)"))
 
         y = sb("y", [P, PACK, N], F32)
         y_codes = sb("y_codes", [P, N], U32)
@@ -194,15 +194,17 @@ def tile_picked_toklearn_sigmoid_po_kernel(tc, x_words, x_scales, wa, wb, gt, gi
         out_rows = out_0.rearrange("(p d) n -> p d n", d=PACK)
 
         def last_product(c):
+            quant(z2_codes[c][:], z2_scales[c][:], z2_bf[c].rearrange("p n t -> p (n t)"))
             acc = bank(c, "out_acc%d" % c)
-            four_passes(acc, z_codes[:], z_scales[:], v_codes[c][:], v_scales[c][:])
-            cols = slice(c * CHUNK, (c + 1) * CHUNK)
+            four_passes(acc, z_codes[:], z_scales[:], z2_codes[c][:], z2_scales[c][:])
+            cols = chunk_cols(c)
             nc.scalar.activation(y[:, :, cols], acc[:], COPY, scale=OUT_SCALE)
             nc.sync.dma_start(out=out_rows[:, :, cols], in_=y[:, :, cols])
 
         y_bf = {}
+        words_out = out_1[0].rearrange("p n r -> p (n r)").bitcast(I32)
 
-        def weave_y(start, width, tag):
+        def weave_y(start, width, tag=""):
             y_bf[start] = sb("y_bf%d" % start, [P, width, PACK], BF16, tag=tag)
             weave(nc.vector.tensor_copy, y_bf[start][:], y[:, :, start : start + width])
 
@@ -211,10 +213,9 @@ def tile_picked_toklearn_sigmoid_po_kernel(tc, x_words, x_scales, wa, wb, gt, gi
             quant(y_codes[:, cols], y_scales[:, cols], y_bf[start][:].rearrange("p n d -> p (n d)"))
             nc.sync.dma_start(out=words_out[:, cols], in_=y_codes[:, cols].bitcast(I32))
 
-        words_out = out_1[0].rearrange("p n r -> p (n r)").bitcast(I32)
         weave_wa(0)
         quant_wa(0)
-        gather_words(1, "wa_bf0")
+        gather_words(1)
         weave_wa(1)
         quant_wa(1)
         for c in range(CHUNKS):
@@ -222,24 +223,25 @@ def tile_picked_toklearn_sigmoid_po_kernel(tc, x_words, x_scales, wa, wb, gt, gi
             gate_z(c)
         for c in range(CHUNKS):
             weave_wb(c)
-        values(0)
+        product_b(0)
         quant(z_codes[:], z_scales[:], z_bf[:].rearrange("p d m t -> p (d m t)"))
-        values(1)
+        product_b(1)
         for c in range(CHUNKS):
-            gate_v(c)
+            gate_z2(c)
             if c + 2 < CHUNKS:
-                values(c + 2)
+                product_b(c + 2)
             if c > 0:
-                quant_v(c - 1)
                 last_product(c - 1)
-        quant_v(CHUNKS - 1)
         last_product(CHUNKS - 1)
-        weave_y(0, HALF, "v_bf1")
-        weave_y(HALF, CHUNK, "")
+        weave_y(0, HALF, tag="z2_bf1")
+        weave_y(HALF, CHUNK)
         quant_y(0, HALF)
-        weave_y(HALF + CHUNK, CHUNK, "")
+        weave_y(HALF + CHUNK, CHUNK)
         quant_y(HALF, CHUNK)
         quant_y(HALF + CHUNK, CHUNK)
-        for q in range(4):
-            eng = nc.scalar if q % 2 else nc.sync
-            eng.dma_start(out=out_2[0, 4 * q : 4 * q + 4, :].bitcast(I32), in_=y_scales[32 * q : 32 * q + 4, :].bitcast(I32))
+        for q in range(P // QUADRANT):
+            queue = nc.scalar if q % 2 else nc.sync
+            queue.dma_start(
+                out=out_2[0, SCALE_ROWS * q : SCALE_ROWS * (q + 1), :].bitcast(I32),
+                in_=y_scales[QUADRANT * q : QUADRANT * q + SCALE_ROWS, :].bitcast(I32),
+            )

from contextlib import ExitStack

import concourse.mybir as mybir

K, T, S, H, N = 512, 2048, 512, 512, 512
FLOPS = 2 * (K * S * H + K * S * N + S * H * N)

F32 = mybir.dt.float32
BF16 = mybir.dt.bfloat16
I32 = mybir.dt.int32
U32 = mybir.dt.uint32
U16 = mybir.dt.uint16
U8 = mybir.dt.uint8
FP8X4 = mybir.dt.float8_e4m3fn_x4
MULT = mybir.AluOpType.mult
SIGMOID = mybir.ActivationFunctionType.Sigmoid
COPY = mybir.ActivationFunctionType.Copy

P = 128
PACK = 4
RUN = 8
QUADRANT = 32
SCALE_ROWS = 4
LIST_ROWS = 16
LINE = 4
CHUNK = 128
CHUNKS = 4
HALF = 2 * CHUNK
OUT_SCALE = 0.0625


def tile_picked_toklearn_sigmoid_po_kernel(tc, x_words, x_scales, wa, wb, gt, gi, offs, val_l, out_0, out_1, out_2):
    nc = tc.nc
    with ExitStack() as ctx:
        keep = ctx.enter_context(tc.tile_pool(name="keep", bufs=1))
        psum = ctx.enter_context(tc.psum_pool(name="psum", bufs=1))

        def sb(name, shape, dtype, pool=keep, tag=""):
            return pool.tile(shape, dtype, name=name, align_bytes=64, tag=tag)

        def bank(b, name):
            return psum.tile([P, PACK, CHUNK], F32, name=name, tag="bank%d" % b)

        lists = [sb("list_a", [P, S // LIST_ROWS], U16), sb("list_b", [P, S // LIST_ROWS], U16)]
        table_scales = sb("table_scales", [P, T], U8)
        ident = sb("ident", [P, P], F32)

        nc.gpsimd.memset(table_scales[:, : T // 2].bitcast(I32), 0)
        nc.vector.memset(table_scales[:, T // 2 :].bitcast(I32), 0)
        with tc.tile_pool(name="setup", bufs=1) as setup:
            zeros = setup.tile([P, P], F32)
            nc.gpsimd.memset(zeros[:], 0.0)
            nc.gpsimd.affine_select(
                out=ident[:], in_=zeros[:], compare_op=mybir.AluOpType.not_equal, fill=1.0, base=0, pattern=[[-1, P]], channel_multiplier=1
            )
        late = ctx.enter_context(tc.tile_pool(name="late", bufs=1))
        gate_rows = sb("gate_rows", [P, P], F32)
        nc.gpsimd.memset(gate_rows[:], 0.0)
        table_words = sb("table_words", [P, T], U32, pool=late)
        pair_tags = ("pair0", "pair1")
        wa_raw = [sb("wa_raw0", [P, PACK, HALF], F32), sb("wa_raw1", [P, PACK, HALF], F32, pool=late, tag=pair_tags[0])]

        def load_wa(u):
            nc.sync.dma_start(out=wa_raw[u][:], in_=wa.rearrange("(p j) c -> p j c", j=PACK)[:, :, u * HALF : (u + 1) * HALF])

        nc.sync.dma_start(lists[0][:], offs)
        nc.sync.dma_start(lists[1][:], val_l)
        load_wa(0)
        for q in range(P // QUADRANT):
            nc.sync.dma_start(
                out=table_scales[QUADRANT * q : QUADRANT * q + SCALE_ROWS, :].bitcast(I32),
                in_=x_scales[0, SCALE_ROWS * q : SCALE_ROWS * (q + 1), :].bitcast(I32),
            )
        nc.sync.dma_start(out=table_words[:].bitcast(I32), in_=x_words[0].rearrange("p c r -> p (c r)").bitcast(I32))
        load_wa(1)
        wb_raw = sb("wb_raw", [P, PACK, N], F32, pool=late)
        nc.sync.dma_start(out=wb_raw[:], in_=wb.rearrange("(p j) c -> p j c", j=PACK))
        for g, gate in enumerate((gt, gi)):
            nc.gpsimd.dma_start(
                out=gate_rows[PACK * g : PACK * (g + 1), :].rearrange("t (q r) -> t q r", r=RUN),
                in_=gate.rearrange("(q t r) o -> t q (r o)", t=PACK, r=RUN),
            )

        warm = sb("warm", [P, 1], F32)
        nc.scalar.activation(warm[:], ident[:, 0:1], SIGMOID)

        picked_scales = [sb("picked_scales%d" % w, [P, S], U8, tag="picked_scales%d" % w) for w in range(2)]
        dealt_scales = [sb("dealt_scales%d" % w, [P, S], U8) for w in range(2)]
        for w in range(2):
            nc.vector.tensor_copy(picked_scales[w][:], table_scales[:].indirect(lists[w][:]))
        for w in range(2):
            nc.vector.tensor_copy(
                dealt_scales[w][:].bitcast(I32).rearrange("p (t q e) -> p t q e", t=PACK, e=RUN // PACK),
                picked_scales[w][:].bitcast(I32).rearrange("p (q t e) -> p t q e", t=PACK, e=RUN // PACK),
            )
        picked_words = [sb("picked_words%d" % w, [P, S], U32) for w in range(2)]

        def gather_words(w):
            nc.vector.tensor_copy(picked_words[w][:].rearrange("p (t q r) -> p q t r", t=PACK, r=RUN), table_words[:].indirect(lists[w][:]))

        gather_words(0)

        gate_bank = bank(2 * CHUNKS - 1, "gate_bank")
        nc.tensor.transpose(gate_bank[:, 0, :], gate_rows[:], ident[:])
        gates = sb("gates", [P, 2 * PACK], F32)
        nc.scalar.copy(gates[:], gate_bank[:, 0, 0 : 2 * PACK])

        def weave(copy, dst, src):
            copy(dst.rearrange("p (c i) j -> p c j i", i=LINE), src.rearrange("p j (c i) -> p c j i", i=LINE))

        def quant(codes, scales, src):
            nc.vector.quantize_mx(out=codes.bitcast(FP8X4), scales=scales, in_=src)

        wa_bf = [sb("wa_bf%d" % u, [P, HALF, PACK], BF16) for u in range(2)]
        wa_codes = [sb("wa_codes0", [P, HALF], U32, tag="picked_scales0"), sb("wa_codes1", [P, HALF], U32)]
        wa_scales = [sb("wa_scales%d" % u, [P, HALF], U8) for u in range(2)]
        wb_bf = {}
        wb_codes = [sb("wb_codes%d" % c, [P, CHUNK], U32) for c in range(CHUNKS)]
        wb_scales = [sb("wb_scales%d" % c, [P, CHUNK], U8) for c in range(CHUNKS)]

        def chunk_cols(c):
            return slice(c * CHUNK, (c + 1) * CHUNK)

        def weave_wa(u):
            weave(nc.scalar.copy, wa_bf[u][:], wa_raw[u][:])

        def quant_wa(u):
            quant(wa_codes[u][:], wa_scales[u][:], wa_bf[u][:].rearrange("p c j -> p (c j)"))

        def weave_wb(c):
            if c % 2 == 0:
                pair = sb("wb_bf%d" % c, [P, 2, CHUNK, PACK], BF16, pool=late, tag=pair_tags[c // 2])
                wb_bf[c], wb_bf[c + 1] = pair[:, 0], pair[:, 1]
            weave(nc.scalar.copy, wb_bf[c], wb_raw[:, :, chunk_cols(c)])

        def four_passes(acc, stationary_codes, stationary_scales, moving_codes, moving_scales):
            for i in range(PACK):
                cols = slice(i * P, (i + 1) * P)
                nc.tensor.matmul_mx(
                    out=acc[:, i, :],
                    lhsT=stationary_codes[:, cols].bitcast(FP8X4),
                    lhsT_scale=stationary_scales[:, cols],
                    rhs=moving_codes.bitcast(FP8X4),
                    rhs_scale=moving_scales,
                    start=True,
                    stop=True,
                )

        sig = {}
        z_bf = sb("z_bf", [P, PACK, P, PACK], BF16)
        z_codes = sb("z_codes", [P, H], U32)
        z_scales = sb("z_scales", [P, H], U8)
        maps = CHUNK // PACK

        def sigmoid_chunk(c):
            acc = bank(c, "a_acc%d" % c)
            cols = chunk_cols(c % 2)
            four_passes(acc, picked_words[0][:], dealt_scales[0][:], wa_codes[c // 2][:, cols], wa_scales[c // 2][:, cols])
            if c % 2 == 0:
                pair = sb("sig%d" % c, [P, 2, PACK, maps, PACK], F32, pool=late, tag=pair_tags[c // 2])
                sig[c], sig[c + 1] = pair[:, 0], pair[:, 1]
            nc.scalar.activation(sig[c], acc[:].rearrange("p t (m d) -> p d m t", d=PACK), SIGMOID)

        def gate_z(c):
            nc.vector.tensor_tensor(
                z_bf[:, :, maps * c : maps * (c + 1), :],
                sig[c],
                gates[:, 0:PACK].unsqueeze(1).unsqueeze(1).to_broadcast([P, PACK, maps, PACK]),
                MULT,
            )

        z2_pairs = [sb("z2_bf%d" % u, [P, 2, CHUNK, PACK], BF16, tag="z2_bf%d" % u) for u in range(2)]
        z2_bf = [z2_pairs[c // 2][:, c % 2] for c in range(CHUNKS)]
        z2_codes = [sb("z2_codes%d" % c, [P, CHUNK], U32) for c in range(CHUNKS)]
        z2_scales = [sb("z2_scales%d" % c, [P, CHUNK], U8) for c in range(CHUNKS)]
        b_acc = {}

        def product_b(c):
            quant(wb_codes[c][:], wb_scales[c][:], wb_bf[c].rearrange("p c j -> p (c j)"))
            b_acc[c] = bank(CHUNKS + c, "b_acc%d" % c)
            four_passes(b_acc[c], picked_words[1][:], dealt_scales[1][:], wb_codes[c][:], wb_scales[c][:])

        def gate_z2(c):
            nc.vector.tensor_tensor(
                z2_bf[c],
                b_acc[c][:].rearrange("p t n -> p n t"),
                gates[:, PACK : 2 * PACK].unsqueeze(1).to_broadcast([P, CHUNK, PACK]),
                MULT,
            )

        y = sb("y", [P, PACK, N], F32)
        y_codes = sb("y_codes", [P, N], U32)
        y_scales = sb("y_scales", [P, N], U8)
        out_rows = out_0.rearrange("(p d) n -> p d n", d=PACK)

        def last_product(c):
            quant(z2_codes[c][:], z2_scales[c][:], z2_bf[c].rearrange("p n t -> p (n t)"))
            acc = bank(c, "out_acc%d" % c)
            four_passes(acc, z_codes[:], z_scales[:], z2_codes[c][:], z2_scales[c][:])
            cols = chunk_cols(c)
            nc.scalar.activation(y[:, :, cols], acc[:], COPY, scale=OUT_SCALE)
            nc.sync.dma_start(out=out_rows[:, :, cols], in_=y[:, :, cols])

        y_bf = {}
        words_out = out_1[0].rearrange("p n r -> p (n r)").bitcast(I32)

        def weave_y(start, width, tag=""):
            y_bf[start] = sb("y_bf%d" % start, [P, width, PACK], BF16, tag=tag)
            weave(nc.vector.tensor_copy, y_bf[start][:], y[:, :, start : start + width])

        def quant_y(start, width):
            cols = slice(start, start + width)
            quant(y_codes[:, cols], y_scales[:, cols], y_bf[start][:].rearrange("p n d -> p (n d)"))
            nc.sync.dma_start(out=words_out[:, cols], in_=y_codes[:, cols].bitcast(I32))

        weave_wa(0)
        quant_wa(0)
        gather_words(1)
        weave_wa(1)
        quant_wa(1)
        for c in range(CHUNKS):
            sigmoid_chunk(c)
            gate_z(c)
        for c in range(CHUNKS):
            weave_wb(c)
        product_b(0)
        quant(z_codes[:], z_scales[:], z_bf[:].rearrange("p d m t -> p (d m t)"))
        product_b(1)
        for c in range(CHUNKS):
            gate_z2(c)
            if c + 2 < CHUNKS:
                product_b(c + 2)
            if c > 0:
                last_product(c - 1)
        last_product(CHUNKS - 1)
        weave_y(0, HALF, tag="z2_bf1")
        weave_y(HALF, CHUNK)
        quant_y(0, HALF)
        weave_y(HALF + CHUNK, CHUNK)
        quant_y(HALF, CHUNK)
        quant_y(HALF + CHUNK, CHUNK)
        for q in range(P // QUADRANT):
            queue = nc.scalar if q % 2 else nc.sync
            queue.dma_start(
                out=out_2[0, SCALE_ROWS * q : SCALE_ROWS * (q + 1), :].bitcast(I32),
                in_=y_scales[QUADRANT * q : QUADRANT * q + SCALE_ROWS, :].bitcast(I32),
            )
